import numpy as np
import ml_dtypes


def mxq(x, axis, fmt="e4m3"):
    dtype, down = {"e4m3": (ml_dtypes.float8_e4m3fn, 7), "e5m2": (ml_dtypes.float8_e5m2, 14)}[fmt]
    v = np.moveaxis(np.asarray(x, np.float32).astype(ml_dtypes.bfloat16).astype(np.float64), axis, -1)
    blocks = v.reshape(v.shape[:-1] + (-1, 32))
    amax = np.abs(blocks).max(-1, keepdims=True)
    byte = np.maximum(np.where(amax > 0, np.frexp(amax)[1] - 1 + 127, 0) - down, 1)
    scale = np.exp2(byte - 127.0)
    codes = (blocks / scale).astype(np.float32).astype(dtype).astype(np.float64)
    return np.moveaxis((codes * scale).reshape(v.shape), -1, axis)


WIDE = False


def mx_kscale(k):
    if not WIDE:
        return np.ones(k)
    levels = np.array([10, -10, 5, -5, 0])
    if k % 512:
        return np.exp2(np.random.permutation(np.resize(levels, k // 32))).repeat(32)
    a = np.empty((k // 512, 16))
    for p in range(k // 512):
        a[p, :8] = np.random.permutation(np.resize(levels, 8))
        for g in range(8):
            far = levels[np.abs(levels - a[p, g]) >= 10]
            a[p, g + 8] = far[np.random.randint(len(far))]
    return np.exp2(a.ravel()).repeat(32)


def f64(x):
    return np.asarray(x).astype(np.float64)


def striped(idx):
    return np.tile(idx.reshape(-1, 16).T, (8, 1)).astype(np.uint16)


def unstriped(offs):
    return offs[:16].T.reshape(-1).astype(np.int64)

def planes(y):
    n, m = y.shape
    v = y.astype(np.float32).astype(ml_dtypes.bfloat16).astype(np.float64).reshape(n // 32, 32, m)
    top = np.abs(v).max(1)
    byte = np.clip(np.where(top > 0, np.frexp(top)[1] - 1 + 127 - 7, 1), 1, 254)
    codes = (v * np.exp2(127.0 - byte)[:, None, :]).reshape(n, m).astype(np.float32).astype(ml_dtypes.float8_e4m3fn).view(np.uint8)
    words = codes.reshape(n // 512, 128, 4, m).transpose(0, 1, 3, 2)
    return np.ascontiguousarray(words), np.ascontiguousarray(byte.astype(np.uint8).reshape(n // 512, 16, m))


K, T, S, N, U = 512, 1024, 512, 512, 1024


def setup_inputs():
    n = np.random.standard_normal
    s = mx_kscale(K)[:, None]
    return {
        "xT": (n((K, T)) * s).astype(np.float32),
        "mem": n((N, U)).astype(np.float32),
        "w1": (n((K, N)) / np.sqrt(K) / s).astype(np.float32),
        "offs": striped(np.random.permutation(T)[:S]),
        "slot": striped(np.random.permutation(U)[:S]),
    }


def reference(xT, mem, w1, offs, slot):
    xq = mxq(f64(xT)[:, unstriped(offs)], 0, "e4m3")
    y = mxq(f64(w1), 0, "e4m3").T @ xq
    out = f64(mem).copy()
    out[:, unstriped(slot)] = y
    return (out,) + planes(out)

@@ -1,0 +1,144 @@
+from contextlib import ExitStack
+
+import concourse.mybir as mybir
+
+K, T, S, N, U = 512, 1024, 512, 512, 1024
+FLOPS = 2 * K * S * N
+
+F32 = mybir.dt.float32
+BF16 = mybir.dt.bfloat16
+I32 = mybir.dt.int32
+U32 = mybir.dt.uint32
+U16 = mybir.dt.uint16
+U8 = mybir.dt.uint8
+FP8X4 = mybir.dt.float8_e4m3fn_x4
+COPY = mybir.ActivationFunctionType.Copy
+
+P = 128
+PACK = 4
+HALF = S // 2
+LIST_HALF = HALF // 16
+W_HALF = N // 2
+M_HALF = W_HALF // PACK
+M_VECTOR = 40
+CHUNK = 256
+CHUNKS = U // CHUNK
+
+
+def tile_picked_kvput_none_lo_kernel(tc, xT, mem, w1, offs, slot, out_0, out_1, out_2):
+    nc = tc.nc
+    x_rows = xT.rearrange("(p j) c -> p j c", j=PACK)
+    w_rows = w1.rearrange("(p j) c -> p j c", j=PACK)
+    mem_rows = mem.rearrange("(p t) c -> p t c", t=PACK)
+    out_rows = out_0.rearrange("(p t) c -> p t c", t=PACK)
+    out_words = out_1[0].rearrange("p c r -> p (c r)").bitcast(I32)
+    out_scales = out_2[0].bitcast(I32)
+
+    with ExitStack() as ctx:
+        keep = ctx.enter_context(tc.tile_pool(name="keep", bufs=1))
+        psum = ctx.enter_context(tc.psum_pool(name="psum", bufs=1))
+
+        offs_sb = keep.tile([P, S // 16], U16, name="offs_sb")
+        slot_sb = keep.tile([P, S // 16], U16, name="slot_sb")
+        x_plane = [keep.tile([P, T], F32, name=f"x_plane{j}") for j in range(PACK)]
+        w_raw = [keep.tile([P, PACK, W_HALF], F32, name=f"w_raw{h}") for h in range(2)]
+        page = [keep.tile([P, U], F32, name=f"page{t}") for t in range(PACK)]
+
+        nc.sync.dma_start(out=x_plane[0][:], in_=x_rows[:, 0, :])
+        nc.sync.dma_start(offs_sb[:], offs)
+        for j in range(1, PACK):
+            nc.sync.dma_start(out=x_plane[j][:], in_=x_rows[:, j, :])
+        for h in range(2):
+            nc.sync.dma_start(out=w_raw[h][:], in_=w_rows[:, :, h * W_HALF:(h + 1) * W_HALF])
+        nc.sync.dma_start(slot_sb[:], slot)
+        for t in (0, 2, 1, 3):
+            nc.sync.dma_start(out=page[t][:], in_=mem_rows[:, t, :])
+
+        x_grouped = [keep.tile([P, HALF, PACK], BF16, name=f"x_grouped{h}", align_bytes=64) for h in range(2)]
+        x_flat = keep.tile([P, PACK, HALF], BF16, name="x_flat")
+        for j in range(PACK):
+            nc.vector.tensor_copy(out=x_grouped[0][:, :, j], in_=x_plane[j][:].indirect(offs_sb[:, 0:LIST_HALF]))
+            nc.scalar.activation(out=x_flat[:, j, :], in_=x_plane[j][:].indirect(offs_sb[:, LIST_HALF:2 * LIST_HALF]), func=COPY)
+        nc.scalar.copy(out=x_grouped[1][:].rearrange("p (c i) j -> p c j i", i=4),
+                       in_=x_flat[:].rearrange("p j (c i) -> p c j i", i=4))
+
+        x_codes = keep.tile([P, S], U32, name="x_codes", align_bytes=64)
+        x_scales = keep.tile([P, S], U8, name="x_scales", align_bytes=64)
+
+        def quantize_x(h):
+            cols = slice(h * HALF, (h + 1) * HALF)
+            nc.vector.quantize_mx(out=x_codes[:, cols].bitcast(FP8X4), scales=x_scales[:, cols],
+                                  in_=x_grouped[h][:].rearrange("p c j -> p (c j)"))
+
+        w_grouped = keep.tile([P, PACK, P, PACK], BF16, name="w_grouped", align_bytes=64)
+
+        def deal_w(copy, h, m0, m1):
+            copy(out=w_grouped[:, :, h * M_HALF + m0:h * M_HALF + m1, :].rearrange("p t m j -> p m t j"),
+                 in_=w_raw[h][:].rearrange("p j (m t) -> p m t j", t=PACK)[:, m0:m1, :, :])
+
+        quantize_x(0)
+        deal_w(nc.vector.tensor_copy, 0, 0, M_HALF)
+        quantize_x(1)
+        deal_w(nc.vector.tensor_copy, 1, 0, M_VECTOR)
+        deal_w(nc.scalar.copy, 1, M_VECTOR, M_HALF)
+
+        w_codes = keep.tile([P, N], U32, name="w_codes", align_bytes=64)
+        w_scales = keep.tile([P, N], U8, name="w_scales", align_bytes=64)
+        y = [keep.tile([P, S], F32, name=f"y{t}", tag=f"y{t}") for t in range(PACK)]
+
+        def product(t, s0, s1):
+            rows = slice(t * P, (t + 1) * P)
+            acc = psum.tile([P, s1 - s0], F32, name=f"acc{t}_{s0}")
+            nc.tensor.matmul_mx(out=acc[:], lhsT=w_codes[:, rows].bitcast(FP8X4), lhsT_scale=w_scales[:, rows],
+                                rhs=x_codes[:, s0:s1].bitcast(FP8X4), rhs_scale=x_scales[:, s0:s1],
+                                start=True, stop=True)
+            nc.scalar.copy(out=y[t][:, s0:s1], in_=acc[:])
+
+        for t in (0, 2, 1, 3):
+            rows = slice(t * P, (t + 1) * P)
+            nc.vector.quantize_mx(out=w_codes[:, rows].bitcast(FP8X4), scales=w_scales[:, rows],
+                                  in_=w_grouped[:, t, :, :].rearrange("p m j -> p (m j)"))
+            if t == 0:
+                product(t, 0, HALF)
+                product(t, HALF, S)
+            else:
+                product(t, 0, S)
+
+        def scatter_vector(t, h):
+            nc.vector.tensor_copy(out=page[t][:].indirect(slot_sb[:, h * LIST_HALF:(h + 1) * LIST_HALF]),
+                                  in_=y[t][:, h * HALF:(h + 1) * HALF])
+
+        def scatter_scalar(t, h):
+            nc.scalar.activation(out=page[t][:].indirect(slot_sb[:, h * LIST_HALF:(h + 1) * LIST_HALF]),
+                                 in_=y[t][:, h * HALF:(h + 1) * HALF], func=COPY)
+
+        for tv, ts in ((0, 2), (1, 3)):
+            for h in range(2):
+                scatter_vector(tv, h)
+                scatter_scalar(ts, h)
+            for t in (tv, ts):
+                nc.sync.dma_start(out=out_rows[:, t, :], in_=page[t][:])
+
+        pairs = keep.tile([P, CHUNKS, 2, CHUNK, 2], BF16, name="pairs", tag="y1")
+        for t in range(PACK - 1):
+            nc.vector.tensor_copy(out=pairs[:, :, t // 2, :, t % 2], in_=page[t][:].rearrange("p (c u) -> p c u", u=CHUNK))
+        for c in range(CHUNKS):
+            nc.vector.tensor_copy(out=pairs[:, c, 1, :, 1], in_=page[3][:, c * CHUNK:(c + 1) * CHUNK])
+
+        o_codes = keep.tile([P, U], U32, name="o_codes", align_bytes=64)
+        o_scales = keep.tile([P, U], U8, name="o_scales", align_bytes=64)
+        o_grouped = [keep.tile([P, CHUNK * PACK], BF16, name=f"o_grouped{c}", align_bytes=64) for c in range(CHUNKS)]
+
+        def weave(copy, dtype, c):
+            copy(out=o_grouped[c][:].bitcast(dtype).rearrange("p (u a) -> p u a", a=2),
+                 in_=pairs[:, c, :, :, :].rearrange("p a u e -> p (a u e)").bitcast(dtype).rearrange("p (a u) -> p u a", a=2))
+
+        for c in range(CHUNKS - 1):
+            weave(nc.scalar.copy, U32, c)
+        weave(nc.vector.tensor_copy, I32, CHUNKS - 1)
+        for c in (0, 3, 1, 2):
+            cols = slice(c * CHUNK, (c + 1) * CHUNK)
+            nc.vector.quantize_mx(out=o_codes[:, cols].bitcast(FP8X4), scales=o_scales[:, cols], in_=o_grouped[c][:])
+            nc.sync.dma_start(out=out_words[:, cols], in_=o_codes[:, cols].bitcast(I32))
+        for q in range(4):
+            nc.scalar.dma_start(out=out_scales[4 * q:4 * q + 4, :], in_=o_scales[32 * q:32 * q + 4, :].bitcast(I32))

@@ -18,9 +18,10 @@ P = 128
 PACK = 4
 HALF = S // 2
 LIST_HALF = HALF // 16
-W_HALF = N // 2
-M_HALF = W_HALF // PACK
-M_VECTOR = 40
+QUARTER = S // 4
+M_VECTOR = 104
+MULT = mybir.AluOpType.mult
+ADD = mybir.AluOpType.add
 CHUNK = 256
 CHUNKS = U // CHUNK
 
@@ -41,88 +42,100 @@ def tile_picked_kvput_none_lo_kernel(tc, xT, mem, w1, offs, slot, out_0, out_1, 
         offs_sb = keep.tile([P, S // 16], U16, name="offs_sb")
         slot_sb = keep.tile([P, S // 16], U16, name="slot_sb")
         x_plane = [keep.tile([P, T], F32, name=f"x_plane{j}") for j in range(PACK)]
-        w_raw = [keep.tile([P, PACK, W_HALF], F32, name=f"w_raw{h}") for h in range(2)]
+        w_raw = keep.tile([P, PACK, N], F32, name="w_raw")
         page = [keep.tile([P, U], F32, name=f"page{t}") for t in range(PACK)]
 
-        nc.sync.dma_start(out=x_plane[0][:], in_=x_rows[:, 0, :])
+        nc.sync.dma_start(out=w_raw[:], in_=w_rows)
         nc.sync.dma_start(offs_sb[:], offs)
-        for j in range(1, PACK):
+        for j in range(PACK):
             nc.sync.dma_start(out=x_plane[j][:], in_=x_rows[:, j, :])
-        for h in range(2):
-            nc.sync.dma_start(out=w_raw[h][:], in_=w_rows[:, :, h * W_HALF:(h + 1) * W_HALF])
         nc.sync.dma_start(slot_sb[:], slot)
-        for t in (0, 2, 1, 3):
+        for t in range(PACK):
             nc.sync.dma_start(out=page[t][:], in_=mem_rows[:, t, :])
+
+        w_grouped = keep.tile([P, PACK, P, PACK], BF16, name="w_grouped", align_bytes=64)
+        w_codes = keep.tile([P, N], U32, name="w_codes", align_bytes=64)
+        w_scales = keep.tile([P, N], U8, name="w_scales", align_bytes=64)
+        for copy, ms in ((nc.vector.tensor_copy, slice(0, M_VECTOR)), (nc.scalar.copy, slice(M_VECTOR, P))):
+            copy(out=w_grouped[:, :, ms, :].rearrange("p t m j -> p m t j"),
+                 in_=w_raw[:].rearrange("p j (m t) -> p m t j", t=PACK)[:, ms, :, :])
+        nc.vector.quantize_mx(out=w_codes[:].bitcast(FP8X4), scales=w_scales[:],
+                              in_=w_grouped[:].rearrange("p t m j -> p (t m j)"))
 
         x_grouped = [keep.tile([P, HALF, PACK], BF16, name=f"x_grouped{h}", align_bytes=64) for h in range(2)]
         x_flat = keep.tile([P, PACK, HALF], BF16, name="x_flat")
-        for j in range(PACK):
-            nc.vector.tensor_copy(out=x_grouped[0][:, :, j], in_=x_plane[j][:].indirect(offs_sb[:, 0:LIST_HALF]))
-            nc.scalar.activation(out=x_flat[:, j, :], in_=x_plane[j][:].indirect(offs_sb[:, LIST_HALF:2 * LIST_HALF]), func=COPY)
-        nc.scalar.copy(out=x_grouped[1][:].rearrange("p (c i) j -> p c j i", i=4),
-                       in_=x_flat[:].rearrange("p j (c i) -> p c j i", i=4))
-
         x_codes = keep.tile([P, S], U32, name="x_codes", align_bytes=64)
         x_scales = keep.tile([P, S], U8, name="x_scales", align_bytes=64)
 
-        def quantize_x(h):
-            cols = slice(h * HALF, (h + 1) * HALF)
+        def gather_vector(j, s0, s1):
+            nc.vector.tensor_copy(out=x_grouped[0][:, s0:s1, j], in_=x_plane[j][:].indirect(offs_sb[:, s0 // 16:s1 // 16]))
+
+        def quantize_x(h, s0, s1):
+            cols = slice(h * HALF + s0, h * HALF + s1)
             nc.vector.quantize_mx(out=x_codes[:, cols].bitcast(FP8X4), scales=x_scales[:, cols],
-                                  in_=x_grouped[h][:].rearrange("p c j -> p (c j)"))
+                                  in_=x_grouped[h][:, s0:s1, :].rearrange("p c j -> p (c j)"))
 
-        w_grouped = keep.tile([P, PACK, P, PACK], BF16, name="w_grouped", align_bytes=64)
+        for j in range(PACK):
+            if j < PACK - 1:
+                gather_vector(j, 0, HALF)
+            else:
+                gather_vector(j, 0, QUARTER)
+                gather_vector(j, QUARTER, HALF)
+            nc.scalar.activation(out=x_flat[:, j, :], in_=x_plane[j][:].indirect(offs_sb[:, LIST_HALF:2 * LIST_HALF]), func=COPY)
+            if j % 2 == 1:
+                nc.scalar.copy(out=x_grouped[1][:, :, j - 1:j + 1], in_=x_flat[:, j - 1:j + 1, :].rearrange("p j c -> p c j"))
+        quantize_x(0, 0, QUARTER)
+        quantize_x(0, QUARTER, HALF)
+        quantize_x(1, 0, HALF)
 
-        def deal_w(copy, h, m0, m1):
-            copy(out=w_grouped[:, :, h * M_HALF + m0:h * M_HALF + m1, :].rearrange("p t m j -> p m t j"),
-                 in_=w_raw[h][:].rearrange("p j (m t) -> p m t j", t=PACK)[:, m0:m1, :, :])
+        y = {}
 
-        quantize_x(0)
-        deal_w(nc.vector.tensor_copy, 0, 0, M_HALF)
-        quantize_x(1)
-        deal_w(nc.vector.tensor_copy, 1, 0, M_VECTOR)
-        deal_w(nc.scalar.copy, 1, M_VECTOR, M_HALF)
-
-        w_codes = keep.tile([P, N], U32, name="w_codes", align_bytes=64)
-        w_scales = keep.tile([P, N], U8, name="w_scales", align_bytes=64)
-        y = [keep.tile([P, S], F32, name=f"y{t}", tag=f"y{t}") for t in range(PACK)]
-
-        def product(t, s0, s1):
+        def product(t, s0, s1, copy, dst):
             rows = slice(t * P, (t + 1) * P)
             acc = psum.tile([P, s1 - s0], F32, name=f"acc{t}_{s0}")
             nc.tensor.matmul_mx(out=acc[:], lhsT=w_codes[:, rows].bitcast(FP8X4), lhsT_scale=w_scales[:, rows],
                                 rhs=x_codes[:, s0:s1].bitcast(FP8X4), rhs_scale=x_scales[:, s0:s1],
                                 start=True, stop=True)
-            nc.scalar.copy(out=y[t][:, s0:s1], in_=acc[:])
+            y[t, s0] = dst
+            copy(out=dst, in_=acc[:])
 
-        for t in (0, 2, 1, 3):
-            rows = slice(t * P, (t + 1) * P)
-            nc.vector.quantize_mx(out=w_codes[:, rows].bitcast(FP8X4), scales=w_scales[:, rows],
-                                  in_=w_grouped[:, t, :, :].rearrange("p m j -> p (m j)"))
-            if t == 0:
-                product(t, 0, HALF)
-                product(t, HALF, S)
-            else:
-                product(t, 0, S)
+        def scatter_vector(t, s0, s1):
+            nc.vector.tensor_copy(out=page[t][:].indirect(slot_sb[:, s0 // 16:s1 // 16]), in_=y[t, s0])
 
-        def scatter_vector(t, h):
-            nc.vector.tensor_copy(out=page[t][:].indirect(slot_sb[:, h * LIST_HALF:(h + 1) * LIST_HALF]),
-                                  in_=y[t][:, h * HALF:(h + 1) * HALF])
+        def scatter_scalar(t, s0, s1):
+            nc.scalar.activation(out=page[t][:].indirect(slot_sb[:, s0 // 16:s1 // 16]), in_=y[t, s0], func=COPY)
 
-        def scatter_scalar(t, h):
-            nc.scalar.activation(out=page[t][:].indirect(slot_sb[:, h * LIST_HALF:(h + 1) * LIST_HALF]),
-                                 in_=y[t][:, h * HALF:(h + 1) * HALF], func=COPY)
+        y_first = keep.tile([P, QUARTER], F32, name="y_first")
+        y_second = keep.tile([P, QUARTER], F32, name="y_second", tag="vector_feed")
+        y_third = keep.tile([P, HALF], F32, name="y_third", tag="scalar_feed")
+        product(0, 0, QUARTER, nc.scalar.copy, y_first[:])
+        product(0, QUARTER, HALF, nc.scalar.copy, y_second[:])
+        product(1, 0, HALF, nc.scalar.copy, y_third[:])
+        scatter_vector(0, 0, QUARTER)
+        scatter_vector(0, QUARTER, HALF)
+        scatter_scalar(1, 0, HALF)
+        y_rest = keep.tile([P, 4 * HALF], F32, name="y_rest", tag="scalar_feed")
+        y_two = keep.tile([P, S], F32, name="y_two", tag="vector_feed")
+        product(0, HALF, S, nc.scalar.copy, y_rest[:, 0:HALF])
+        product(1, HALF, S, nc.scalar.copy, y_rest[:, HALF:2 * HALF])
+        product(2, 0, S, nc.vector.tensor_copy, y_two[:])
+        product(3, 0, S, nc.scalar.copy, y_rest[:, 2 * HALF:4 * HALF])
+        y[3, HALF] = y_rest[:, 3 * HALF:4 * HALF]
+        y[3, 0] = y_rest[:, 2 * HALF:3 * HALF]
+        scatter_vector(0, HALF, S)
+        scatter_scalar(1, HALF, S)
+        scatter_vector(2, 0, S)
+        scatter_scalar(3, 0, HALF)
+        scatter_scalar(3, HALF, S)
+        for t in range(PACK):
+            nc.sync.dma_start(out=out_rows[:, t, :], in_=page[t][:])
 
-        for tv, ts in ((0, 2), (1, 3)):
-            for h in range(2):
-                scatter_vector(tv, h)
-                scatter_scalar(ts, h)
-            for t in (tv, ts):
-                nc.sync.dma_start(out=out_rows[:, t, :], in_=page[t][:])
-
-        pairs = keep.tile([P, CHUNKS, 2, CHUNK, 2], BF16, name="pairs", tag="y1")
-        for t in range(PACK - 1):
-            nc.vector.tensor_copy(out=pairs[:, :, t // 2, :, t % 2], in_=page[t][:].rearrange("p (c u) -> p c u", u=CHUNK))
-        for c in range(CHUNKS):
+        pairs = keep.tile([P, CHUNKS, 2, CHUNK, 2], BF16, name="pairs")
+        for t in range(2):
+            nc.gpsimd.tensor_scalar(out=pairs[:, :, 0, :, t], in0=page[t][:].rearrange("p (c u) -> p c u", u=CHUNK),
+                                    scalar1=1.0, scalar2=-0.0, op0=MULT, op1=ADD)
+        nc.vector.tensor_copy(out=pairs[:, :, 1, :, 0], in_=page[2][:].rearrange("p (c u) -> p c u", u=CHUNK))
+        for c in (0, 2, 1, 3):
             nc.vector.tensor_copy(out=pairs[:, c, 1, :, 1], in_=page[3][:, c * CHUNK:(c + 1) * CHUNK])
 
         o_codes = keep.tile([P, U], U32, name="o_codes", align_bytes=64)
@@ -133,10 +146,11 @@ def tile_picked_kvput_none_lo_kernel(tc, xT, mem, w1, offs, slot, out_0, out_1, 
             copy(out=o_grouped[c][:].bitcast(dtype).rearrange("p (u a) -> p u a", a=2),
                  in_=pairs[:, c, :, :, :].rearrange("p a u e -> p (a u e)").bitcast(dtype).rearrange("p (a u) -> p u a", a=2))
 
-        for c in range(CHUNKS - 1):
+        for c in (0, 1):
             weave(nc.scalar.copy, U32, c)
-        weave(nc.vector.tensor_copy, I32, CHUNKS - 1)
-        for c in (0, 3, 1, 2):
+        for c in (2, 3):
+            weave(nc.vector.tensor_copy, I32, c)
+        for c in (0, 2, 3, 1):
             cols = slice(c * CHUNK, (c + 1) * CHUNK)
             nc.vector.quantize_mx(out=o_codes[:, cols].bitcast(FP8X4), scales=o_scales[:, cols], in_=o_grouped[c][:])
             nc.sync.dma_start(out=out_words[:, cols], in_=o_codes[:, cols].bitcast(I32))

@@ -19,7 +19,7 @@ PACK = 4
 HALF = S // 2
 LIST_HALF = HALF // 16
 QUARTER = S // 4
-M_VECTOR = 104
+M_VECTOR = 88
 MULT = mybir.AluOpType.mult
 ADD = mybir.AluOpType.add
 CHUNK = 256
@@ -82,10 +82,11 @@ def tile_picked_kvput_none_lo_kernel(tc, xT, mem, w1, offs, slot, out_0, out_1, 
                 gather_vector(j, 0, QUARTER)
                 gather_vector(j, QUARTER, HALF)
             nc.scalar.activation(out=x_flat[:, j, :], in_=x_plane[j][:].indirect(offs_sb[:, LIST_HALF:2 * LIST_HALF]), func=COPY)
-            if j % 2 == 1:
-                nc.scalar.copy(out=x_grouped[1][:, :, j - 1:j + 1], in_=x_flat[:, j - 1:j + 1, :].rearrange("p j c -> p c j"))
+            if j == 1:
+                nc.scalar.copy(out=x_grouped[1][:, :, 0:2], in_=x_flat[:, 0:2, :].rearrange("p j c -> p c j"))
         quantize_x(0, 0, QUARTER)
         quantize_x(0, QUARTER, HALF)
+        nc.vector.tensor_copy(out=x_grouped[1][:, :, 2:4], in_=x_flat[:, 2:4, :].rearrange("p j c -> p c j"))
         quantize_x(1, 0, HALF)
 
         y = {}
@@ -109,8 +110,8 @@ def tile_picked_kvput_none_lo_kernel(tc, xT, mem, w1, offs, slot, out_0, out_1, 
         y_second = keep.tile([P, QUARTER], F32, name="y_second", tag="vector_feed")
         y_third = keep.tile([P, HALF], F32, name="y_third", tag="scalar_feed")
         product(0, 0, QUARTER, nc.scalar.copy, y_first[:])
-        product(0, QUARTER, HALF, nc.scalar.copy, y_second[:])
         product(1, 0, HALF, nc.scalar.copy, y_third[:])
+        product(0, QUARTER, HALF, nc.scalar.copy, y_second[:])
         scatter_vector(0, 0, QUARTER)
         scatter_vector(0, QUARTER, HALF)
         scatter_scalar(1, 0, HALF)
@@ -155,4 +156,5 @@ def tile_picked_kvput_none_lo_kernel(tc, xT, mem, w1, offs, slot, out_0, out_1, 
             nc.vector.quantize_mx(out=o_codes[:, cols].bitcast(FP8X4), scales=o_scales[:, cols], in_=o_grouped[c][:])
             nc.sync.dma_start(out=out_words[:, cols], in_=o_codes[:, cols].bitcast(I32))
         for q in range(4):
-            nc.scalar.dma_start(out=out_scales[4 * q:4 * q + 4, :], in_=o_scales[32 * q:32 * q + 4, :].bitcast(I32))
+            queue = nc.scalar if q < 2 else nc.sync
+            queue.dma_start(out=out_scales[4 * q:4 * q + 4, :], in_=o_scales[32 * q:32 * q + 4, :].bitcast(I32))

@@ -19,7 +19,7 @@ PACK = 4
 HALF = S // 2
 LIST_HALF = HALF // 16
 QUARTER = S // 4
-M_VECTOR = 88
+M_VECTOR = 84
 MULT = mybir.AluOpType.mult
 ADD = mybir.AluOpType.add
 CHUNK = 256
@@ -42,10 +42,11 @@ def tile_picked_kvput_none_lo_kernel(tc, xT, mem, w1, offs, slot, out_0, out_1, 
         offs_sb = keep.tile([P, S // 16], U16, name="offs_sb")
         slot_sb = keep.tile([P, S // 16], U16, name="slot_sb")
         x_plane = [keep.tile([P, T], F32, name=f"x_plane{j}") for j in range(PACK)]
-        w_raw = keep.tile([P, PACK, N], F32, name="w_raw")
+        w_raw = [keep.tile([P, 2, N], F32, name=f"w_raw{h}") for h in range(2)]
         page = [keep.tile([P, U], F32, name=f"page{t}") for t in range(PACK)]
 
-        nc.sync.dma_start(out=w_raw[:], in_=w_rows)
+        for h in range(2):
+            nc.sync.dma_start(out=w_raw[h][:], in_=w_rows[:, 2 * h:2 * h + 2, :])
         nc.sync.dma_start(offs_sb[:], offs)
         for j in range(PACK):
             nc.sync.dma_start(out=x_plane[j][:], in_=x_rows[:, j, :])
@@ -56,9 +57,14 @@ def tile_picked_kvput_none_lo_kernel(tc, xT, mem, w1, offs, slot, out_0, out_1, 
         w_grouped = keep.tile([P, PACK, P, PACK], BF16, name="w_grouped", align_bytes=64)
         w_codes = keep.tile([P, N], U32, name="w_codes", align_bytes=64)
         w_scales = keep.tile([P, N], U8, name="w_scales", align_bytes=64)
-        for copy, ms in ((nc.vector.tensor_copy, slice(0, M_VECTOR)), (nc.scalar.copy, slice(M_VECTOR, P))):
-            copy(out=w_grouped[:, :, ms, :].rearrange("p t m j -> p m t j"),
-                 in_=w_raw[:].rearrange("p j (m t) -> p m t j", t=PACK)[:, ms, :, :])
+
+        def deal_w(copy, h, m0, m1):
+            copy(out=w_grouped[:, :, m0:m1, 2 * h:2 * h + 2].rearrange("p t (a b) j -> p a t b j", b=2),
+                 in_=w_raw[h][:, :, m0 * PACK:m1 * PACK].rearrange("p j (a b t) -> p a t b j", b=2, t=PACK))
+
+        deal_w(nc.vector.tensor_copy, 0, 0, P)
+        deal_w(nc.vector.tensor_copy, 1, 0, M_VECTOR)
+        deal_w(nc.scalar.copy, 1, M_VECTOR, P)
         nc.vector.quantize_mx(out=w_codes[:].bitcast(FP8X4), scales=w_scales[:],
                               in_=w_grouped[:].rearrange("p t m j -> p (t m j)"))
 

from contextlib import ExitStack

import concourse.mybir as mybir

K, T, S, N, U = 512, 1024, 512, 512, 1024
FLOPS = 2 * K * S * N

F32 = mybir.dt.float32
BF16 = mybir.dt.bfloat16
I32 = mybir.dt.int32
U32 = mybir.dt.uint32
U16 = mybir.dt.uint16
U8 = mybir.dt.uint8
FP8X4 = mybir.dt.float8_e4m3fn_x4
COPY = mybir.ActivationFunctionType.Copy

P = 128
PACK = 4
HALF = S // 2
LIST_HALF = HALF // 16
QUARTER = S // 4
M_VECTOR = 84
MULT = mybir.AluOpType.mult
ADD = mybir.AluOpType.add
CHUNK = 256
CHUNKS = U // CHUNK


def tile_picked_kvput_none_lo_kernel(tc, xT, mem, w1, offs, slot, out_0, out_1, out_2):
    nc = tc.nc
    x_rows = xT.rearrange("(p j) c -> p j c", j=PACK)
    w_rows = w1.rearrange("(p j) c -> p j c", j=PACK)
    mem_rows = mem.rearrange("(p t) c -> p t c", t=PACK)
    out_rows = out_0.rearrange("(p t) c -> p t c", t=PACK)
    out_words = out_1[0].rearrange("p c r -> p (c r)").bitcast(I32)
    out_scales = out_2[0].bitcast(I32)

    with ExitStack() as ctx:
        keep = ctx.enter_context(tc.tile_pool(name="keep", bufs=1))
        psum = ctx.enter_context(tc.psum_pool(name="psum", bufs=1))

        offs_sb = keep.tile([P, S // 16], U16, name="offs_sb")
        slot_sb = keep.tile([P, S // 16], U16, name="slot_sb")
        x_plane = [keep.tile([P, T], F32, name=f"x_plane{j}") for j in range(PACK)]
        w_raw = [keep.tile([P, 2, N], F32, name=f"w_raw{h}") for h in range(2)]
        page = [keep.tile([P, U], F32, name=f"page{t}") for t in range(PACK)]

        for h in range(2):
            nc.sync.dma_start(out=w_raw[h][:], in_=w_rows[:, 2 * h:2 * h + 2, :])
        nc.sync.dma_start(offs_sb[:], offs)
        for j in range(PACK):
            nc.sync.dma_start(out=x_plane[j][:], in_=x_rows[:, j, :])
        nc.sync.dma_start(slot_sb[:], slot)
        for t in range(PACK):
            nc.sync.dma_start(out=page[t][:], in_=mem_rows[:, t, :])

        w_grouped = keep.tile([P, PACK, P, PACK], BF16, name="w_grouped", align_bytes=64)
        w_codes = keep.tile([P, N], U32, name="w_codes", align_bytes=64)
        w_scales = keep.tile([P, N], U8, name="w_scales", align_bytes=64)

        def deal_w(copy, h, m0, m1):
            copy(out=w_grouped[:, :, m0:m1, 2 * h:2 * h + 2].rearrange("p t (a b) j -> p a t b j", b=2),
                 in_=w_raw[h][:, :, m0 * PACK:m1 * PACK].rearrange("p j (a b t) -> p a t b j", b=2, t=PACK))

        deal_w(nc.vector.tensor_copy, 0, 0, P)
        deal_w(nc.vector.tensor_copy, 1, 0, M_VECTOR)
        deal_w(nc.scalar.copy, 1, M_VECTOR, P)
        nc.vector.quantize_mx(out=w_codes[:].bitcast(FP8X4), scales=w_scales[:],
                              in_=w_grouped[:].rearrange("p t m j -> p (t m j)"))

        x_grouped = [keep.tile([P, HALF, PACK], BF16, name=f"x_grouped{h}", align_bytes=64) for h in range(2)]
        x_flat = keep.tile([P, PACK, HALF], BF16, name="x_flat")
        x_codes = keep.tile([P, S], U32, name="x_codes", align_bytes=64)
        x_scales = keep.tile([P, S], U8, name="x_scales", align_bytes=64)

        def gather_vector(j, s0, s1):
            nc.vector.tensor_copy(out=x_grouped[0][:, s0:s1, j], in_=x_plane[j][:].indirect(offs_sb[:, s0 // 16:s1 // 16]))

        def quantize_x(h, s0, s1):
            cols = slice(h * HALF + s0, h * HALF + s1)
            nc.vector.quantize_mx(out=x_codes[:, cols].bitcast(FP8X4), scales=x_scales[:, cols],
                                  in_=x_grouped[h][:, s0:s1, :].rearrange("p c j -> p (c j)"))

        for j in range(PACK):
            if j < PACK - 1:
                gather_vector(j, 0, HALF)
            else:
                gather_vector(j, 0, QUARTER)
                gather_vector(j, QUARTER, HALF)
            nc.scalar.activation(out=x_flat[:, j, :], in_=x_plane[j][:].indirect(offs_sb[:, LIST_HALF:2 * LIST_HALF]), func=COPY)
            if j == 1:
                nc.scalar.copy(out=x_grouped[1][:, :, 0:2], in_=x_flat[:, 0:2, :].rearrange("p j c -> p c j"))
        quantize_x(0, 0, QUARTER)
        quantize_x(0, QUARTER, HALF)
        nc.vector.tensor_copy(out=x_grouped[1][:, :, 2:4], in_=x_flat[:, 2:4, :].rearrange("p j c -> p c j"))
        quantize_x(1, 0, HALF)

        y = {}

        def product(t, s0, s1, copy, dst):
            rows = slice(t * P, (t + 1) * P)
            acc = psum.tile([P, s1 - s0], F32, name=f"acc{t}_{s0}")
            nc.tensor.matmul_mx(out=acc[:], lhsT=w_codes[:, rows].bitcast(FP8X4), lhsT_scale=w_scales[:, rows],
                                rhs=x_codes[:, s0:s1].bitcast(FP8X4), rhs_scale=x_scales[:, s0:s1],
                                start=True, stop=True)
            y[t, s0] = dst
            copy(out=dst, in_=acc[:])

        def scatter_vector(t, s0, s1):
            nc.vector.tensor_copy(out=page[t][:].indirect(slot_sb[:, s0 // 16:s1 // 16]), in_=y[t, s0])

        def scatter_scalar(t, s0, s1):
            nc.scalar.activation(out=page[t][:].indirect(slot_sb[:, s0 // 16:s1 // 16]), in_=y[t, s0], func=COPY)

        y_first = keep.tile([P, QUARTER], F32, name="y_first")
        y_second = keep.tile([P, QUARTER], F32, name="y_second", tag="vector_feed")
        y_third = keep.tile([P, HALF], F32, name="y_third", tag="scalar_feed")
        product(0, 0, QUARTER, nc.scalar.copy, y_first[:])
        product(1, 0, HALF, nc.scalar.copy, y_third[:])
        product(0, QUARTER, HALF, nc.scalar.copy, y_second[:])
        scatter_vector(0, 0, QUARTER)
        scatter_vector(0, QUARTER, HALF)
        scatter_scalar(1, 0, HALF)
        y_rest = keep.tile([P, 4 * HALF], F32, name="y_rest", tag="scalar_feed")
        y_two = keep.tile([P, S], F32, name="y_two", tag="vector_feed")
        product(0, HALF, S, nc.scalar.copy, y_rest[:, 0:HALF])
        product(1, HALF, S, nc.scalar.copy, y_rest[:, HALF:2 * HALF])
        product(2, 0, S, nc.vector.tensor_copy, y_two[:])
        product(3, 0, S, nc.scalar.copy, y_rest[:, 2 * HALF:4 * HALF])
        y[3, HALF] = y_rest[:, 3 * HALF:4 * HALF]
        y[3, 0] = y_rest[:, 2 * HALF:3 * HALF]
        scatter_vector(0, HALF, S)
        scatter_scalar(1, HALF, S)
        scatter_vector(2, 0, S)
        scatter_scalar(3, 0, HALF)
        scatter_scalar(3, HALF, S)
        for t in range(PACK):
            nc.sync.dma_start(out=out_rows[:, t, :], in_=page[t][:])

        pairs = keep.tile([P, CHUNKS, 2, CHUNK, 2], BF16, name="pairs")
        for t in range(2):
            nc.gpsimd.tensor_scalar(out=pairs[:, :, 0, :, t], in0=page[t][:].rearrange("p (c u) -> p c u", u=CHUNK),
                                    scalar1=1.0, scalar2=-0.0, op0=MULT, op1=ADD)
        nc.vector.tensor_copy(out=pairs[:, :, 1, :, 0], in_=page[2][:].rearrange("p (c u) -> p c u", u=CHUNK))
        for c in (0, 2, 1, 3):
            nc.vector.tensor_copy(out=pairs[:, c, 1, :, 1], in_=page[3][:, c * CHUNK:(c + 1) * CHUNK])

        o_codes = keep.tile([P, U], U32, name="o_codes", align_bytes=64)
        o_scales = keep.tile([P, U], U8, name="o_scales", align_bytes=64)
        o_grouped = [keep.tile([P, CHUNK * PACK], BF16, name=f"o_grouped{c}", align_bytes=64) for c in range(CHUNKS)]

        def weave(copy, dtype, c):
            copy(out=o_grouped[c][:].bitcast(dtype).rearrange("p (u a) -> p u a", a=2),
                 in_=pairs[:, c, :, :, :].rearrange("p a u e -> p (a u e)").bitcast(dtype).rearrange("p (a u) -> p u a", a=2))

        for c in (0, 1):
            weave(nc.scalar.copy, U32, c)
        for c in (2, 3):
            weave(nc.vector.tensor_copy, I32, c)
        for c in (0, 2, 3, 1):
            cols = slice(c * CHUNK, (c + 1) * CHUNK)
            nc.vector.quantize_mx(out=o_codes[:, cols].bitcast(FP8X4), scales=o_scales[:, cols], in_=o_grouped[c][:])
            nc.sync.dma_start(out=out_words[:, cols], in_=o_codes[:, cols].bitcast(I32))
        for q in range(4):
            queue = nc.scalar if q < 2 else nc.sync
            queue.dma_start(out=out_scales[4 * q:4 * q + 4, :], in_=o_scales[32 * q:32 * q + 4, :].bitcast(I32))
